import numpy as np
import ml_dtypes


def mxq(x, axis, fmt="e4m3"):
    dtype, down = {"e4m3": (ml_dtypes.float8_e4m3fn, 7), "e5m2": (ml_dtypes.float8_e5m2, 14)}[fmt]
    v = np.moveaxis(np.asarray(x, np.float32).astype(ml_dtypes.bfloat16).astype(np.float64), axis, -1)
    blocks = v.reshape(v.shape[:-1] + (-1, 32))
    amax = np.abs(blocks).max(-1, keepdims=True)
    byte = np.maximum(np.where(amax > 0, np.frexp(amax)[1] - 1 + 127, 0) - down, 1)
    scale = np.exp2(byte - 127.0)
    codes = (blocks / scale).astype(np.float32).astype(dtype).astype(np.float64)
    return np.moveaxis((codes * scale).reshape(v.shape), -1, axis)


WIDE = False


def mx_kscale(k):
    if not WIDE:
        return np.ones(k)
    levels = np.array([10, -10, 5, -5, 0])
    if k % 512:
        return np.exp2(np.random.permutation(np.resize(levels, k // 32))).repeat(32)
    a = np.empty((k // 512, 16))
    for p in range(k // 512):
        a[p, :8] = np.random.permutation(np.resize(levels, 8))
        for g in range(8):
            far = levels[np.abs(levels - a[p, g]) >= 10]
            a[p, g + 8] = far[np.random.randint(len(far))]
    return np.exp2(a.ravel()).repeat(32)


def f64(x):
    return np.asarray(x).astype(np.float64)


def striped(idx):
    return np.tile(np.asarray(idx).reshape(-1, 16).T, (8, 1)).astype(np.uint16)


def unstriped(offs):
    return offs[:16].T.reshape(-1).astype(np.int64)


E2M1 = np.array([0.0, 0.5, 1.0, 1.5, 2.0, 3.0, 4.0, 6.0, -0.0, -0.5, -1.0, -1.5, -2.0, -3.0, -4.0, -6.0])


def pack_weight(w, fmt):
    k, n = w.shape
    w = f64(np.asarray(w, np.float32).astype(ml_dtypes.bfloat16)).reshape(k // 32, 32, n)
    amax = np.abs(w).max(1)
    if fmt == "e4m3":
        byte = np.frexp(amax)[1] - 1 + 127 - 7
    else:
        mant, ex = np.frexp(amax / 6.0)
        byte = np.where(mant > 0.5, ex, ex - 1) + 127
    byte = np.clip(np.where(amax > 0, byte, 1), 1, 254)
    scaled = (w * np.exp2(127.0 - byte)[:, None, :]).reshape(k, n).astype(np.float32)
    by_word = np.ascontiguousarray(scaled.reshape(k // 512, 128, 4, n).transpose(0, 1, 3, 2))
    if fmt == "e4m3":
        words = by_word.astype(ml_dtypes.float8_e4m3fn).view(np.uint8)
    else:
        c = by_word.astype(ml_dtypes.float4_e2m1fn).view(np.uint8) & 0xF
        words = (c[..., 0::2] | (c[..., 1::2] << 4)).reshape(k // 512, 128, 2 * n)
    return np.ascontiguousarray(words), np.ascontiguousarray(byte.astype(np.uint8).reshape(k // 512, 16, n))


def unpack_weight(words, scales, fmt):
    g, _, n = scales.shape
    words = np.ascontiguousarray(words).reshape(g, 128, n, -1)
    if fmt == "e4m3":
        vals = words.view(ml_dtypes.float8_e4m3fn).astype(np.float64)
    else:
        nib = np.empty((g, 128, n, 4), np.uint8)
        nib[..., 0::2] = words & 0xF
        nib[..., 1::2] = words >> 4
        vals = E2M1[nib]
    vals = vals * np.repeat(np.exp2(scales.astype(np.float64) - 127.0), 8, axis=1)[..., None]
    return vals.transpose(0, 1, 3, 2).reshape(g * 512, n)


def bf(x):
    return np.asarray(x, np.float32).astype(ml_dtypes.bfloat16)


def planes(Y):
    r, m = Y.shape
    b = f64(bf(Y)).reshape(r // 32, 32, m)
    amax = np.abs(b).max(1)
    byte = np.clip(np.where(amax > 0, np.frexp(amax)[1] - 1 + 127 - 7, 1), 1, 254)
    codes = (b * np.exp2(127.0 - byte)[:, None, :]).reshape(r, m).astype(np.float32).astype(ml_dtypes.float8_e4m3fn).view(np.uint8)
    words = codes.reshape(r // 512, 128, 4, m).transpose(0, 1, 3, 2)
    return np.ascontiguousarray(words), np.ascontiguousarray(byte.astype(np.uint8).reshape(r // 512, 16, m))


D, T, I, Q, E, U, M = 512, 2048, 512, 256, 512, 1024, 1024


def setup_inputs():
    n = np.random.standard_normal
    idx = np.random.permutation(T)[:I]
    idx2 = np.random.permutation(U)[:I]
    idx3 = np.random.permutation(M)[:Q]
    fd = mx_kscale(D)
    fi = mx_kscale(I)
    ti = np.ones(T)
    ti[idx] = fi
    keysp = pack_weight(n((D, T)) / fd[:, None], "e2m1")
    return {
        "query": (n((D, Q)) * 0.7 / np.sqrt(D) * fd[:, None]).astype(np.float32),
        "query2": (n((D, Q)) * 0.7 / np.sqrt(D) * fd[:, None]).astype(np.float32),
        "keys_words": keysp[0],
        "keys_scales": keysp[1],
        "notes": (n((D, U)) / fd[:, None]).astype(np.float32),
        "os": (np.random.uniform(0.02, 0.08, (1, I)) * fi).astype(np.float32),
        "vals": (n((E, T)) / ti).astype(np.float32),
        "member": (n((E, M))).astype(np.float32),
        "mgain": np.tile(np.random.uniform(0.5, 2.0, M), (128, 1)).astype(np.float32),
        "offs": striped(idx),
        "offs2": striped(idx2),
        "offs3": striped(idx3),
    }


def reference(query, query2, keys_words, keys_scales, notes, os, vals, member, mgain, offs, offs2, offs3):
    idx = unstriped(offs)
    idx2 = unstriped(offs2)
    idx3 = unstriped(offs3)
    keysu = unpack_weight(keys_words, keys_scales, "e2m1")
    queryq = mxq(f64(query), 0, "e4m3")
    keysidxg = keysu[:, idx]
    query2q = mxq(f64(query2), 0, "e4m3")
    notesidx2q = mxq(f64(notes)[:, idx2], 0, "e4m3")
    s = queryq.T @ keysidxg + query2q.T @ notesidx2q
    w = np.maximum(s, 0.0)
    wo1 = w * f64(os)
    wt1 = wo1.T
    vt1 = f64(vals)[:, idx].T
    vt1q = mxq(vt1, 0, "e4m3")
    wt1q = mxq(wt1, 0, "e4m3")
    o = vt1q.T @ wt1q
    y = o * f64(mgain)[:1][:, idx3] + f64(member)[:, idx3]
    words, scales = planes(y)
    return y, words, scales

@@ -1,0 +1,205 @@
+from contextlib import ExitStack
+
+import concourse.mybir as mybir
+from concourse.masks import make_identity
+
+D, T, I, Q, E, U, M = 512, 2048, 512, 256, 512, 1024, 1024
+FLOPS = 2 * Q * I * D * 2 + 2 * E * Q * I
+BYTES = 4 * (2 * D * Q + D * U + I + E * T + E * M + M + E * Q) + D * T // 2 + 16 * T + 256 * (32 + 32 + 16) + E * Q + 16 * Q
+
+F32 = mybir.dt.float32
+BF16 = mybir.dt.bfloat16
+I32 = mybir.dt.int32
+U32 = mybir.dt.uint32
+U16 = mybir.dt.uint16
+U8 = mybir.dt.uint8
+FP8X4 = mybir.dt.float8_e4m3fn_x4
+FP4X4 = mybir.dt.float4_e2m1fn_x4
+ALU = mybir.AluOpType
+COPY = mybir.ActivationFunctionType.Copy
+
+P = 128
+PACK = 4
+HALF = 128
+RUN = 4
+
+
+def tile_attend_twosources_bymember_lean_pl_kernel(
+    tc, query, query2, keys_words, keys_scales, notes, slot_factor, vals, member, mgain,
+    offs, offs2, offs3, out_0, out_1, out_2,
+):
+    nc = tc.nc
+    with ExitStack() as ctx:
+        held = ctx.enter_context(tc.tile_pool(name="held", bufs=1))
+        psum = ctx.enter_context(tc.psum_pool(name="psum", bufs=2))
+        banks = ctx.enter_context(tc.psum_pool(name="banks", bufs=1))
+
+        def keep(shape, dtype, name):
+            return held.tile(shape, dtype, name=name, align_bytes=64)
+
+        def planes_of(table, width, name):
+            rows = table.rearrange("(p j) c -> j p c", j=PACK)
+            return [(keep([P, width], F32, "%s%d" % (name, j)), rows[j]) for j in range(PACK)]
+
+        def quantize(grouped, words, name):
+            codes = keep([P, words], U32, name + "_codes")
+            scales = keep([P, words], U8, name + "_scales")
+            nc.vector.quantize_mx(out=codes[:].bitcast(FP8X4), scales=scales[:], in_=grouped)
+            return codes, scales
+
+        slots = keep([P, I // 16], U16, "slots")
+        slots2 = keep([P, I // 16], U16, "slots2")
+        rows3 = keep([P, Q // 16], U16, "rows3")
+        key_words = keep([P, T], U16, "key_words")
+        key_bytes = keep([P, T], U8, "key_bytes")
+        note_planes = planes_of(notes, U, "notes")
+        val_planes = planes_of(vals, T, "vals")
+        member_planes = planes_of(member, M, "member")
+        q_raw = keep([P, PACK, Q], F32, "q_raw")
+        q2_raw = keep([P, PACK, Q], F32, "q2_raw")
+        factor = keep([P, 1, PACK], F32, "factor")
+        gain_cols = keep([P, M // P], F32, "gain_cols")
+        ident = keep([P, P], F32, "ident")
+
+        nc.vector.memset(key_bytes[:].bitcast(I32), 0)
+        make_identity(nc, ident[:])
+
+        nc.sync.dma_start(key_words[:].bitcast(I32), keys_words[0].bitcast(I32))
+        nc.sync.dma_start(slots[:], offs)
+        nc.sync.dma_start(gain_cols[:], mgain[0:1, :].rearrange("o (p j) -> (o p) j", p=P))
+        nc.sync.dma_start(slots2[:], offs2)
+        for tile, rows in note_planes[:3]:
+            nc.sync.dma_start(tile[:], rows)
+        for quad in range(4):
+            nc.sync.dma_start(
+                key_bytes[32 * quad : 32 * quad + 4, :].bitcast(I32),
+                keys_scales[0, 4 * quad : 4 * quad + 4, :].bitcast(I32),
+            )
+        for tile, rows in note_planes[3:]:
+            nc.sync.dma_start(tile[:], rows)
+        nc.sync.dma_start(q2_raw[:], query2.rearrange("(p j) q -> p j q", j=PACK))
+        nc.sync.dma_start(q_raw[:], query.rearrange("(p j) q -> p j q", j=PACK))
+        nc.sync.dma_start(rows3[:], offs3)
+        nc.sync.dma_start(factor[:], slot_factor.rearrange("o (p t) -> p o t", t=PACK))
+        for tile, rows in val_planes + member_planes:
+            nc.sync.dma_start(tile[:], rows)
+
+        kw_listed = keep([P, I], U16, "kw_listed")
+        nc.vector.tensor_copy(kw_listed[:], key_words[:].indirect(slots[:]))
+        k_scales = keep([P, I], U8, "k_scales")
+        nc.vector.tensor_copy(
+            k_scales[:].rearrange("p (r s) -> p s r", r=PACK), key_bytes[:].indirect(slots[:])
+        )
+        k_codes = keep([P, I], U16, "k_codes")
+        nc.vector.tensor_copy(
+            k_codes[:].rearrange("p (r s) -> p s r", r=PACK),
+            kw_listed[:].rearrange("p (s r) -> p s r", r=PACK),
+        )
+
+        gain_row = keep([P, M], F32, "gain_row")
+        per_bank = 4
+        for b in range(M // P // per_bank):
+            spread = psum.tile([P, per_bank, P], F32, name="spread")
+            for jj in range(per_bank):
+                j = per_bank * b + jj
+                nc.tensor.transpose(spread[:, jj, :], gain_cols[:, j : j + 1].to_broadcast([P, P]), ident[:])
+            nc.scalar.copy(
+                gain_row[:].rearrange("p (k b jj) -> p k b jj", jj=per_bank, k=P)[:, :, b, :],
+                spread[:].rearrange("p jj k -> p k jj"),
+            )
+
+        n_listed = keep([P, PACK, I], BF16, "n_listed")
+        for j, (tile, rows) in enumerate(note_planes):
+            if j % 2 == 0:
+                nc.scalar.activation(n_listed[:, j, :], tile[:].indirect(slots2[:]), COPY)
+            else:
+                nc.vector.tensor_copy(n_listed[:, j, :], tile[:].indirect(slots2[:]))
+        n_grouped = keep([P, I * PACK], BF16, "n_grouped")
+        nc.vector.tensor_copy(
+            n_grouped[:].rearrange("p (r s j) -> p s j r", r=PACK, j=PACK),
+            n_listed[:].rearrange("p j (s r) -> p s j r", r=PACK),
+        )
+
+        grouped = []
+        for raw, name in ((q2_raw, "q2"), (q_raw, "q")):
+            g = keep([P, Q * PACK], BF16, name + "_grouped")
+            nc.scalar.copy(
+                g[:].rearrange("p (c i j) -> p c j i", i=RUN, j=PACK),
+                raw[:].rearrange("p j (c i) -> p c j i", i=RUN),
+            )
+            grouped.append(g)
+        n_codes, n_scales = quantize(n_grouped[:], I, "n")
+        q2_codes, q2_scales = quantize(grouped[0][:], Q, "q2")
+        q_codes, q_scales = quantize(grouped[1][:], Q, "q")
+
+        gain = keep([P, 1, Q], F32, "gain")
+        nc.scalar.activation(gain[:, 0, :], gain_row[:].indirect(rows3[:]), COPY)
+
+        w_grouped = keep([P, Q * PACK], BF16, "w_grouped")
+        for h in range(Q // HALF):
+            cols = slice(h * HALF, (h + 1) * HALF)
+            score = psum.tile([P, PACK, HALF], F32, name="score")
+            for r in range(PACK):
+                st = slice(r * P, (r + 1) * P)
+                nc.tensor.matmul_mx(
+                    out=score[:, r, :], lhsT=k_codes[:, st].bitcast(FP4X4), lhsT_scale=k_scales[:, st],
+                    rhs=q_codes[:, cols].bitcast(FP8X4), rhs_scale=q_scales[:, cols], start=True, stop=False,
+                )
+                nc.tensor.matmul_mx(
+                    out=score[:, r, :], lhsT=n_codes[:, st].bitcast(FP8X4), lhsT_scale=n_scales[:, st],
+                    rhs=q2_codes[:, cols].bitcast(FP8X4), rhs_scale=q2_scales[:, cols], start=False, stop=True,
+                )
+            nc.vector.scalar_tensor_tensor(
+                out=w_grouped[:, h * HALF * PACK : (h + 1) * HALF * PACK].rearrange("p (q r) -> p q r", r=PACK),
+                in0=score[:].rearrange("p r q -> p q r"),
+                scalar=0.0,
+                in1=factor[:].to_broadcast([P, HALF, PACK]),
+                op0=ALU.max,
+                op1=ALU.mult,
+            )
+        w_codes, w_scales = quantize(w_grouped[:], Q, "w")
+
+        v_quant = []
+        for j, (tile, rows) in enumerate(val_planes):
+            v_listed = keep([P, I], BF16, "v_listed%d" % j)
+            nc.scalar.activation(v_listed[:], tile[:].indirect(slots[:]), COPY)
+            pairs = v_listed[:].bitcast(F32)
+            turned = banks.tile([P, 2, P], F32, name="turned%d" % j, tag="bank%d" % (j % 2))
+            for u in range(2):
+                nc.tensor.transpose(turned[:, u, :], pairs[:, u : I // 2 : 2], ident[:])
+            v_grouped = keep([P, P * PACK], BF16, "v_grouped%d" % j)
+            nc.vector.tensor_copy(
+                v_grouped[:].bitcast(F32).rearrange("p (e u) -> p e u", u=2),
+                turned[:].rearrange("p u e -> p e u"),
+            )
+            v_quant.append(quantize(v_grouped[:], P, "v%d" % j))
+
+        y = keep([P, PACK, Q], F32, "y")
+        y_rows = out_0.rearrange("(p j) q -> j p q", j=PACK)
+        for planes, tag in (((0, 1), "bank0"), ((2,), "bank2"), ((3,), "bank1")):
+            count = len(planes)
+            mixed = banks.tile([P, count, Q], F32, name="mixed%d" % planes[0], tag=tag)
+            for jj, j in enumerate(planes):
+                v_codes, v_scales = v_quant[j]
+                nc.tensor.matmul_mx(
+                    out=mixed[:, jj, :], lhsT=v_codes[:].bitcast(FP8X4), lhsT_scale=v_scales[:],
+                    rhs=w_codes[:].bitcast(FP8X4), rhs_scale=w_scales[:], start=True, stop=True,
+                )
+            o_gain = keep([P, count, Q], F32, "o_gain%d" % planes[0])
+            nc.vector.tensor_tensor(o_gain[:], mixed[:], gain[:].to_broadcast([P, count, Q]), ALU.mult)
+            for jj, j in enumerate(planes):
+                nc.vector.tensor_tensor(y[:, j, :], member_planes[j][0][:].indirect(rows3[:]), o_gain[:, jj, :], ALU.add)
+                nc.sync.dma_start(y_rows[j], y[:, j, :])
+        y_grouped = keep([P, Q * PACK], BF16, "y_grouped")
+        nc.vector.tensor_copy(
+            y_grouped[:].rearrange("p (c i j) -> p c j i", i=RUN, j=PACK),
+            y[:].rearrange("p j (c i) -> p c j i", i=RUN),
+        )
+        y_codes, y_scales = quantize(y_grouped[:], Q, "y")
+        nc.sync.dma_start(out_1[0].rearrange("p c t -> p (c t)").bitcast(I32), y_codes[:].bitcast(I32))
+        for quad in range(4):
+            queue = nc.scalar if quad % 2 == 0 else nc.sync
+            queue.dma_start(
+                out_2[0, 4 * quad : 4 * quad + 4, :].bitcast(I32),
+                y_scales[32 * quad : 32 * quad + 4, :].bitcast(I32),
+            )

@@ -68,20 +68,16 @@ def tile_attend_twosources_bymember_lean_pl_kernel(
         nc.sync.dma_start(slots[:], offs)
         nc.sync.dma_start(gain_cols[:], mgain[0:1, :].rearrange("o (p j) -> (o p) j", p=P))
         nc.sync.dma_start(slots2[:], offs2)
-        for tile, rows in note_planes[:3]:
+        for tile, rows in note_planes:
             nc.sync.dma_start(tile[:], rows)
-        for quad in range(4):
-            nc.sync.dma_start(
-                key_bytes[32 * quad : 32 * quad + 4, :].bitcast(I32),
-                keys_scales[0, 4 * quad : 4 * quad + 4, :].bitcast(I32),
-            )
-        for tile, rows in note_planes[3:]:
-            nc.sync.dma_start(tile[:], rows)
+        for r in range(4):
+            nc.sync.dma_start(key_bytes[r:P:32, :].bitcast(I32), keys_scales[0, r:16:4, :].bitcast(I32))
         nc.sync.dma_start(q2_raw[:], query2.rearrange("(p j) q -> p j q", j=PACK))
         nc.sync.dma_start(q_raw[:], query.rearrange("(p j) q -> p j q", j=PACK))
-        nc.sync.dma_start(rows3[:], offs3)
+        nc.sync.dma_start(val_planes[0][0][:], val_planes[0][1])
         nc.sync.dma_start(factor[:], slot_factor.rearrange("o (p t) -> p o t", t=PACK))
-        for tile, rows in val_planes + member_planes:
+        nc.sync.dma_start(rows3[:], offs3)
+        for tile, rows in val_planes[1:] + member_planes:
             nc.sync.dma_start(tile[:], rows)
 
         kw_listed = keep([P, I], U16, "kw_listed")
@@ -132,9 +128,6 @@ def tile_attend_twosources_bymember_lean_pl_kernel(
         q2_codes, q2_scales = quantize(grouped[0][:], Q, "q2")
         q_codes, q_scales = quantize(grouped[1][:], Q, "q")
 
-        gain = keep([P, 1, Q], F32, "gain")
-        nc.scalar.activation(gain[:, 0, :], gain_row[:].indirect(rows3[:]), COPY)
-
         w_grouped = keep([P, Q * PACK], BF16, "w_grouped")
         for h in range(Q // HALF):
             cols = slice(h * HALF, (h + 1) * HALF)
@@ -159,12 +152,11 @@ def tile_attend_twosources_bymember_lean_pl_kernel(
             )
         w_codes, w_scales = quantize(w_grouped[:], Q, "w")
 
-        v_quant = []
-        for j, (tile, rows) in enumerate(val_planes):
+        def values(j, tag):
             v_listed = keep([P, I], BF16, "v_listed%d" % j)
-            nc.scalar.activation(v_listed[:], tile[:].indirect(slots[:]), COPY)
+            nc.scalar.activation(v_listed[:], val_planes[j][0][:].indirect(slots[:]), COPY)
             pairs = v_listed[:].bitcast(F32)
-            turned = banks.tile([P, 2, P], F32, name="turned%d" % j, tag="bank%d" % (j % 2))
+            turned = banks.tile([P, 2, P], F32, name="turned%d" % j, tag=tag)
             for u in range(2):
                 nc.tensor.transpose(turned[:, u, :], pairs[:, u : I // 2 : 2], ident[:])
             v_grouped = keep([P, P * PACK], BF16, "v_grouped%d" % j)
@@ -172,30 +164,61 @@ def tile_attend_twosources_bymember_lean_pl_kernel(
                 v_grouped[:].bitcast(F32).rearrange("p (e u) -> p e u", u=2),
                 turned[:].rearrange("p u e -> p e u"),
             )
-            v_quant.append(quantize(v_grouped[:], P, "v%d" % j))
+            return quantize(v_grouped[:], P, "v%d" % j)
 
-        y = keep([P, PACK, Q], F32, "y")
-        y_rows = out_0.rearrange("(p j) q -> j p q", j=PACK)
-        for planes, tag in (((0, 1), "bank0"), ((2,), "bank2"), ((3,), "bank1")):
-            count = len(planes)
-            mixed = banks.tile([P, count, Q], F32, name="mixed%d" % planes[0], tag=tag)
-            for jj, j in enumerate(planes):
-                v_codes, v_scales = v_quant[j]
+        o_gain = keep([P, PACK, Q], F32, "o_gain")
+
+        def mix(first, quantized, tag):
+            count = len(quantized)
+            mixed = banks.tile([P, count, Q], F32, name="mixed%d" % first, tag=tag)
+            for jj, (v_codes, v_scales) in enumerate(quantized):
                 nc.tensor.matmul_mx(
                     out=mixed[:, jj, :], lhsT=v_codes[:].bitcast(FP8X4), lhsT_scale=v_scales[:],
                     rhs=w_codes[:].bitcast(FP8X4), rhs_scale=w_scales[:], start=True, stop=True,
                 )
-            o_gain = keep([P, count, Q], F32, "o_gain%d" % planes[0])
-            nc.vector.tensor_tensor(o_gain[:], mixed[:], gain[:].to_broadcast([P, count, Q]), ALU.mult)
-            for jj, j in enumerate(planes):
-                nc.vector.tensor_tensor(y[:, j, :], member_planes[j][0][:].indirect(rows3[:]), o_gain[:, jj, :], ALU.add)
-                nc.sync.dma_start(y_rows[j], y[:, j, :])
+            nc.vector.tensor_tensor(
+                o_gain[:, first : first + count, :], mixed[:], gain[:].to_broadcast([P, count, Q]), ALU.mult
+            )
+
+        first = values(0, "bank0")
+        gain = keep([P, 1, Q], F32, "gain")
+        nc.scalar.activation(gain[:, 0, :], gain_row[:].indirect(rows3[:]), COPY)
+        mix(0, [first, values(1, "bank1")], "bank1")
+        mix(2, [values(2, "bank0")], "bank0")
+        mix(3, [values(3, "bank2")], "bank2")
+
+        y = keep([P, PACK, Q], F32, "y")
+        y_rows = out_0.rearrange("(p j) q -> p j q", j=PACK)
+        last = PACK - 1
+        m_listed = keep([P, last, Q], F32, "m_listed")
+        for j in range(last):
+            nc.scalar.activation(m_listed[:, j, :], member_planes[j][0][:].indirect(rows3[:]), COPY)
+        for planes in (slice(0, 2), slice(2, last)):
+            nc.vector.tensor_tensor(y[:, planes, :], m_listed[:, planes, :], o_gain[:, planes, :], ALU.add)
+            nc.sync.dma_start(y_rows[:, planes, :], y[:, planes, :])
         y_grouped = keep([P, Q * PACK], BF16, "y_grouped")
-        nc.vector.tensor_copy(
-            y_grouped[:].rearrange("p (c i j) -> p c j i", i=RUN, j=PACK),
-            y[:].rearrange("p j (c i) -> p c j i", i=RUN),
-        )
-        y_codes, y_scales = quantize(y_grouped[:], Q, "y")
+        y_codes = keep([P, Q], U32, "y_codes")
+        y_scales = keep([P, Q], U8, "y_scales")
+        halves = [slice(h * HALF, (h + 1) * HALF) for h in range(Q // HALF)]
+        for h, cols in enumerate(halves):
+            nc.vector.tensor_tensor(
+                y[:, last, cols],
+                member_planes[last][0][:].indirect(rows3[:, h * HALF // 16 : (h + 1) * HALF // 16]),
+                o_gain[:, last, cols],
+                ALU.add,
+            )
+        nc.sync.dma_start(y_rows[:, last, :], y[:, last, :])
+        for cols, copy in zip(halves, (nc.scalar.copy, nc.vector.tensor_copy)):
+            copy(
+                y_grouped[:, cols.start * PACK : cols.stop * PACK].rearrange("p (c i j) -> p c j i", i=RUN, j=PACK),
+                y[:, :, cols].rearrange("p j (c i) -> p c j i", i=RUN),
+            )
+        for cols in halves:
+            nc.vector.quantize_mx(
+                out=y_codes[:, cols].bitcast(FP8X4),
+                scales=y_scales[:, cols],
+                in_=y_grouped[:, cols.start * PACK : cols.stop * PACK],
+            )
         nc.sync.dma_start(out_1[0].rearrange("p c t -> p (c t)").bitcast(I32), y_codes[:].bitcast(I32))
         for quad in range(4):
             queue = nc.scalar if quad % 2 == 0 else nc.sync

@@ -61,17 +61,19 @@ def tile_attend_twosources_bymember_lean_pl_kernel(
         gain_cols = keep([P, M // P], F32, "gain_cols")
         ident = keep([P, P], F32, "ident")
 
-        nc.vector.memset(key_bytes[:].bitcast(I32), 0)
+        nc.gpsimd.memset(key_bytes[:].bitcast(I32), 0)
         make_identity(nc, ident[:])
 
         nc.sync.dma_start(key_words[:].bitcast(I32), keys_words[0].bitcast(I32))
         nc.sync.dma_start(slots[:], offs)
-        nc.sync.dma_start(gain_cols[:], mgain[0:1, :].rearrange("o (p j) -> (o p) j", p=P))
         nc.sync.dma_start(slots2[:], offs2)
-        for tile, rows in note_planes:
+        nc.sync.dma_start(gain_cols[:], mgain[0:1, :].rearrange("o (p j) -> (o p) j", p=P))
+        for tile, rows in note_planes[:2]:
             nc.sync.dma_start(tile[:], rows)
         for r in range(4):
             nc.sync.dma_start(key_bytes[r:P:32, :].bitcast(I32), keys_scales[0, r:16:4, :].bitcast(I32))
+        for tile, rows in note_planes[2:]:
+            nc.sync.dma_start(tile[:], rows)
         nc.sync.dma_start(q2_raw[:], query2.rearrange("(p j) q -> p j q", j=PACK))
         nc.sync.dma_start(q_raw[:], query.rearrange("(p j) q -> p j q", j=PACK))
         nc.sync.dma_start(val_planes[0][0][:], val_planes[0][1])
@@ -92,21 +94,9 @@ def tile_attend_twosources_bymember_lean_pl_kernel(
             kw_listed[:].rearrange("p (s r) -> p s r", r=PACK),
         )
 
-        gain_row = keep([P, M], F32, "gain_row")
-        per_bank = 4
-        for b in range(M // P // per_bank):
-            spread = psum.tile([P, per_bank, P], F32, name="spread")
-            for jj in range(per_bank):
-                j = per_bank * b + jj
-                nc.tensor.transpose(spread[:, jj, :], gain_cols[:, j : j + 1].to_broadcast([P, P]), ident[:])
-            nc.scalar.copy(
-                gain_row[:].rearrange("p (k b jj) -> p k b jj", jj=per_bank, k=P)[:, :, b, :],
-                spread[:].rearrange("p jj k -> p k jj"),
-            )
-
         n_listed = keep([P, PACK, I], BF16, "n_listed")
         for j, (tile, rows) in enumerate(note_planes):
-            if j % 2 == 0:
+            if j < 2:
                 nc.scalar.activation(n_listed[:, j, :], tile[:].indirect(slots2[:]), COPY)
             else:
                 nc.vector.tensor_copy(n_listed[:, j, :], tile[:].indirect(slots2[:]))
@@ -128,19 +118,34 @@ def tile_attend_twosources_bymember_lean_pl_kernel(
         q2_codes, q2_scales = quantize(grouped[0][:], Q, "q2")
         q_codes, q_scales = quantize(grouped[1][:], Q, "q")
 
+        gain_row = held.tile([P, M], F32, name="gain_row", tag="q_grouped", align_bytes=64)
+        per_bank = 4
+        for b in range(M // P // per_bank):
+            spread = psum.tile([P, per_bank, P], F32, name="spread")
+            for jj in range(per_bank):
+                j = per_bank * b + jj
+                nc.tensor.transpose(spread[:, jj, :], gain_cols[:, j : j + 1].to_broadcast([P, P]), ident[:])
+            nc.vector.tensor_copy(
+                gain_row[:].rearrange("p (k b jj) -> p k b jj", jj=per_bank, k=P)[:, :, b, :],
+                spread[:].rearrange("p jj k -> p k jj"),
+            )
+
         w_grouped = keep([P, Q * PACK], BF16, "w_grouped")
-        for h in range(Q // HALF):
-            cols = slice(h * HALF, (h + 1) * HALF)
-            score = psum.tile([P, PACK, HALF], F32, name="score")
+        halves = [slice(h * HALF, (h + 1) * HALF) for h in range(Q // HALF)]
+        scores = [psum.tile([P, PACK, HALF], F32, name="score") for cols in halves]
+        for score, cols in zip(scores, halves):
+            for r in range(PACK):
+                st = slice(r * P, (r + 1) * P)
+                nc.tensor.matmul_mx(
+                    out=score[:, r, :], lhsT=n_codes[:, st].bitcast(FP8X4), lhsT_scale=n_scales[:, st],
+                    rhs=q2_codes[:, cols].bitcast(FP8X4), rhs_scale=q2_scales[:, cols], start=(r == 0), stop=False,
+                )
+        for h, (score, cols) in enumerate(zip(scores, halves)):
             for r in range(PACK):
                 st = slice(r * P, (r + 1) * P)
                 nc.tensor.matmul_mx(
                     out=score[:, r, :], lhsT=k_codes[:, st].bitcast(FP4X4), lhsT_scale=k_scales[:, st],
-                    rhs=q_codes[:, cols].bitcast(FP8X4), rhs_scale=q_scales[:, cols], start=True, stop=False,
-                )
-                nc.tensor.matmul_mx(
-                    out=score[:, r, :], lhsT=n_codes[:, st].bitcast(FP8X4), lhsT_scale=n_scales[:, st],
-                    rhs=q2_codes[:, cols].bitcast(FP8X4), rhs_scale=q2_scales[:, cols], start=False, stop=True,
+                    rhs=q_codes[:, cols].bitcast(FP8X4), rhs_scale=q_scales[:, cols], start=False, stop=(r == PACK - 1),
                 )
             nc.vector.scalar_tensor_tensor(
                 out=w_grouped[:, h * HALF * PACK : (h + 1) * HALF * PACK].rearrange("p (q r) -> p q r", r=PACK),
@@ -199,7 +204,6 @@ def tile_attend_twosources_bymember_lean_pl_kernel(
         y_grouped = keep([P, Q * PACK], BF16, "y_grouped")
         y_codes = keep([P, Q], U32, "y_codes")
         y_scales = keep([P, Q], U8, "y_scales")
-        halves = [slice(h * HALF, (h + 1) * HALF) for h in range(Q // HALF)]
         for h, cols in enumerate(halves):
             nc.vector.tensor_tensor(
                 y[:, last, cols],

@@ -52,7 +52,8 @@ def tile_attend_twosources_bymember_lean_pl_kernel(
         rows3 = keep([P, Q // 16], U16, "rows3")
         key_words = keep([P, T], U16, "key_words")
         key_bytes = keep([P, T], U8, "key_bytes")
-        note_planes = planes_of(notes, U, "notes")
+        note_rows = notes.rearrange("(p g j) u -> g p j u", g=2, j=2)
+        note_pairs = [keep([P, 2, U], F32, "notes%d" % g) for g in range(2)]
         val_planes = planes_of(vals, T, "vals")
         member_planes = planes_of(member, M, "member")
         q_raw = keep([P, PACK, Q], F32, "q_raw")
@@ -68,12 +69,10 @@ def tile_attend_twosources_bymember_lean_pl_kernel(
         nc.sync.dma_start(slots[:], offs)
         nc.sync.dma_start(slots2[:], offs2)
         nc.sync.dma_start(gain_cols[:], mgain[0:1, :].rearrange("o (p j) -> (o p) j", p=P))
-        for tile, rows in note_planes[:2]:
-            nc.sync.dma_start(tile[:], rows)
+        nc.sync.dma_start(note_pairs[0][:], note_rows[0])
         for r in range(4):
             nc.sync.dma_start(key_bytes[r:P:32, :].bitcast(I32), keys_scales[0, r:16:4, :].bitcast(I32))
-        for tile, rows in note_planes[2:]:
-            nc.sync.dma_start(tile[:], rows)
+        nc.sync.dma_start(note_pairs[1][:], note_rows[1])
         nc.sync.dma_start(q2_raw[:], query2.rearrange("(p j) q -> p j q", j=PACK))
         nc.sync.dma_start(q_raw[:], query.rearrange("(p j) q -> p j q", j=PACK))
         nc.sync.dma_start(val_planes[0][0][:], val_planes[0][1])
@@ -94,12 +93,10 @@ def tile_attend_twosources_bymember_lean_pl_kernel(
             kw_listed[:].rearrange("p (s r) -> p s r", r=PACK),
         )
 
-        n_listed = keep([P, PACK, I], BF16, "n_listed")
-        for j, (tile, rows) in enumerate(note_planes):
-            if j < 2:
-                nc.scalar.activation(n_listed[:, j, :], tile[:].indirect(slots2[:]), COPY)
-            else:
-                nc.vector.tensor_copy(n_listed[:, j, :], tile[:].indirect(slots2[:]))
+        n_listed = keep([P, PACK, I], F32, "n_listed")
+        for g in range(2):
+            nc.scalar.activation(n_listed[:, 2 * g, :], note_pairs[g][:, 0, :].indirect(slots2[:]), COPY)
+            nc.vector.tensor_copy(n_listed[:, 2 * g + 1, :], note_pairs[g][:, 1, :].indirect(slots2[:]))
         n_grouped = keep([P, I * PACK], BF16, "n_grouped")
         nc.vector.tensor_copy(
             n_grouped[:].rearrange("p (r s j) -> p s j r", r=PACK, j=PACK),

from contextlib import ExitStack

import concourse.mybir as mybir
from concourse.masks import make_identity

D, T, I, Q, E, U, M = 512, 2048, 512, 256, 512, 1024, 1024
FLOPS = 2 * Q * I * D * 2 + 2 * E * Q * I
BYTES = 4 * (2 * D * Q + D * U + I + E * T + E * M + M + E * Q) + D * T // 2 + 16 * T + 256 * (32 + 32 + 16) + E * Q + 16 * Q

F32 = mybir.dt.float32
BF16 = mybir.dt.bfloat16
I32 = mybir.dt.int32
U32 = mybir.dt.uint32
U16 = mybir.dt.uint16
U8 = mybir.dt.uint8
FP8X4 = mybir.dt.float8_e4m3fn_x4
FP4X4 = mybir.dt.float4_e2m1fn_x4
ALU = mybir.AluOpType
COPY = mybir.ActivationFunctionType.Copy

P = 128
PACK = 4
HALF = 128
RUN = 4


def tile_attend_twosources_bymember_lean_pl_kernel(
    tc, query, query2, keys_words, keys_scales, notes, slot_factor, vals, member, mgain,
    offs, offs2, offs3, out_0, out_1, out_2,
):
    nc = tc.nc
    with ExitStack() as ctx:
        held = ctx.enter_context(tc.tile_pool(name="held", bufs=1))
        psum = ctx.enter_context(tc.psum_pool(name="psum", bufs=2))
        banks = ctx.enter_context(tc.psum_pool(name="banks", bufs=1))

        def keep(shape, dtype, name):
            return held.tile(shape, dtype, name=name, align_bytes=64)

        def planes_of(table, width, name):
            rows = table.rearrange("(p j) c -> j p c", j=PACK)
            return [(keep([P, width], F32, "%s%d" % (name, j)), rows[j]) for j in range(PACK)]

        def quantize(grouped, words, name):
            codes = keep([P, words], U32, name + "_codes")
            scales = keep([P, words], U8, name + "_scales")
            nc.vector.quantize_mx(out=codes[:].bitcast(FP8X4), scales=scales[:], in_=grouped)
            return codes, scales

        slots = keep([P, I // 16], U16, "slots")
        slots2 = keep([P, I // 16], U16, "slots2")
        rows3 = keep([P, Q // 16], U16, "rows3")
        key_words = keep([P, T], U16, "key_words")
        key_bytes = keep([P, T], U8, "key_bytes")
        note_rows = notes.rearrange("(p g j) u -> g p j u", g=2, j=2)
        note_pairs = [keep([P, 2, U], F32, "notes%d" % g) for g in range(2)]
        val_planes = planes_of(vals, T, "vals")
        member_planes = planes_of(member, M, "member")
        q_raw = keep([P, PACK, Q], F32, "q_raw")
        q2_raw = keep([P, PACK, Q], F32, "q2_raw")
        factor = keep([P, 1, PACK], F32, "factor")
        gain_cols = keep([P, M // P], F32, "gain_cols")
        ident = keep([P, P], F32, "ident")

        nc.gpsimd.memset(key_bytes[:].bitcast(I32), 0)
        make_identity(nc, ident[:])

        nc.sync.dma_start(key_words[:].bitcast(I32), keys_words[0].bitcast(I32))
        nc.sync.dma_start(slots[:], offs)
        nc.sync.dma_start(slots2[:], offs2)
        nc.sync.dma_start(gain_cols[:], mgain[0:1, :].rearrange("o (p j) -> (o p) j", p=P))
        nc.sync.dma_start(note_pairs[0][:], note_rows[0])
        for r in range(4):
            nc.sync.dma_start(key_bytes[r:P:32, :].bitcast(I32), keys_scales[0, r:16:4, :].bitcast(I32))
        nc.sync.dma_start(note_pairs[1][:], note_rows[1])
        nc.sync.dma_start(q2_raw[:], query2.rearrange("(p j) q -> p j q", j=PACK))
        nc.sync.dma_start(q_raw[:], query.rearrange("(p j) q -> p j q", j=PACK))
        nc.sync.dma_start(val_planes[0][0][:], val_planes[0][1])
        nc.sync.dma_start(factor[:], slot_factor.rearrange("o (p t) -> p o t", t=PACK))
        nc.sync.dma_start(rows3[:], offs3)
        for tile, rows in val_planes[1:] + member_planes:
            nc.sync.dma_start(tile[:], rows)

        kw_listed = keep([P, I], U16, "kw_listed")
        nc.vector.tensor_copy(kw_listed[:], key_words[:].indirect(slots[:]))
        k_scales = keep([P, I], U8, "k_scales")
        nc.vector.tensor_copy(
            k_scales[:].rearrange("p (r s) -> p s r", r=PACK), key_bytes[:].indirect(slots[:])
        )
        k_codes = keep([P, I], U16, "k_codes")
        nc.vector.tensor_copy(
            k_codes[:].rearrange("p (r s) -> p s r", r=PACK),
            kw_listed[:].rearrange("p (s r) -> p s r", r=PACK),
        )

        n_listed = keep([P, PACK, I], F32, "n_listed")
        for g in range(2):
            nc.scalar.activation(n_listed[:, 2 * g, :], note_pairs[g][:, 0, :].indirect(slots2[:]), COPY)
            nc.vector.tensor_copy(n_listed[:, 2 * g + 1, :], note_pairs[g][:, 1, :].indirect(slots2[:]))
        n_grouped = keep([P, I * PACK], BF16, "n_grouped")
        nc.vector.tensor_copy(
            n_grouped[:].rearrange("p (r s j) -> p s j r", r=PACK, j=PACK),
            n_listed[:].rearrange("p j (s r) -> p s j r", r=PACK),
        )

        grouped = []
        for raw, name in ((q2_raw, "q2"), (q_raw, "q")):
            g = keep([P, Q * PACK], BF16, name + "_grouped")
            nc.scalar.copy(
                g[:].rearrange("p (c i j) -> p c j i", i=RUN, j=PACK),
                raw[:].rearrange("p j (c i) -> p c j i", i=RUN),
            )
            grouped.append(g)
        n_codes, n_scales = quantize(n_grouped[:], I, "n")
        q2_codes, q2_scales = quantize(grouped[0][:], Q, "q2")
        q_codes, q_scales = quantize(grouped[1][:], Q, "q")

        gain_row = held.tile([P, M], F32, name="gain_row", tag="q_grouped", align_bytes=64)
        per_bank = 4
        for b in range(M // P // per_bank):
            spread = psum.tile([P, per_bank, P], F32, name="spread")
            for jj in range(per_bank):
                j = per_bank * b + jj
                nc.tensor.transpose(spread[:, jj, :], gain_cols[:, j : j + 1].to_broadcast([P, P]), ident[:])
            nc.vector.tensor_copy(
                gain_row[:].rearrange("p (k b jj) -> p k b jj", jj=per_bank, k=P)[:, :, b, :],
                spread[:].rearrange("p jj k -> p k jj"),
            )

        w_grouped = keep([P, Q * PACK], BF16, "w_grouped")
        halves = [slice(h * HALF, (h + 1) * HALF) for h in range(Q // HALF)]
        scores = [psum.tile([P, PACK, HALF], F32, name="score") for cols in halves]
        for score, cols in zip(scores, halves):
            for r in range(PACK):
                st = slice(r * P, (r + 1) * P)
                nc.tensor.matmul_mx(
                    out=score[:, r, :], lhsT=n_codes[:, st].bitcast(FP8X4), lhsT_scale=n_scales[:, st],
                    rhs=q2_codes[:, cols].bitcast(FP8X4), rhs_scale=q2_scales[:, cols], start=(r == 0), stop=False,
                )
        for h, (score, cols) in enumerate(zip(scores, halves)):
            for r in range(PACK):
                st = slice(r * P, (r + 1) * P)
                nc.tensor.matmul_mx(
                    out=score[:, r, :], lhsT=k_codes[:, st].bitcast(FP4X4), lhsT_scale=k_scales[:, st],
                    rhs=q_codes[:, cols].bitcast(FP8X4), rhs_scale=q_scales[:, cols], start=False, stop=(r == PACK - 1),
                )
            nc.vector.scalar_tensor_tensor(
                out=w_grouped[:, h * HALF * PACK : (h + 1) * HALF * PACK].rearrange("p (q r) -> p q r", r=PACK),
                in0=score[:].rearrange("p r q -> p q r"),
                scalar=0.0,
                in1=factor[:].to_broadcast([P, HALF, PACK]),
                op0=ALU.max,
                op1=ALU.mult,
            )
        w_codes, w_scales = quantize(w_grouped[:], Q, "w")

        def values(j, tag):
            v_listed = keep([P, I], BF16, "v_listed%d" % j)
            nc.scalar.activation(v_listed[:], val_planes[j][0][:].indirect(slots[:]), COPY)
            pairs = v_listed[:].bitcast(F32)
            turned = banks.tile([P, 2, P], F32, name="turned%d" % j, tag=tag)
            for u in range(2):
                nc.tensor.transpose(turned[:, u, :], pairs[:, u : I // 2 : 2], ident[:])
            v_grouped = keep([P, P * PACK], BF16, "v_grouped%d" % j)
            nc.vector.tensor_copy(
                v_grouped[:].bitcast(F32).rearrange("p (e u) -> p e u", u=2),
                turned[:].rearrange("p u e -> p e u"),
            )
            return quantize(v_grouped[:], P, "v%d" % j)

        o_gain = keep([P, PACK, Q], F32, "o_gain")

        def mix(first, quantized, tag):
            count = len(quantized)
            mixed = banks.tile([P, count, Q], F32, name="mixed%d" % first, tag=tag)
            for jj, (v_codes, v_scales) in enumerate(quantized):
                nc.tensor.matmul_mx(
                    out=mixed[:, jj, :], lhsT=v_codes[:].bitcast(FP8X4), lhsT_scale=v_scales[:],
                    rhs=w_codes[:].bitcast(FP8X4), rhs_scale=w_scales[:], start=True, stop=True,
                )
            nc.vector.tensor_tensor(
                o_gain[:, first : first + count, :], mixed[:], gain[:].to_broadcast([P, count, Q]), ALU.mult
            )

        first = values(0, "bank0")
        gain = keep([P, 1, Q], F32, "gain")
        nc.scalar.activation(gain[:, 0, :], gain_row[:].indirect(rows3[:]), COPY)
        mix(0, [first, values(1, "bank1")], "bank1")
        mix(2, [values(2, "bank0")], "bank0")
        mix(3, [values(3, "bank2")], "bank2")

        y = keep([P, PACK, Q], F32, "y")
        y_rows = out_0.rearrange("(p j) q -> p j q", j=PACK)
        last = PACK - 1
        m_listed = keep([P, last, Q], F32, "m_listed")
        for j in range(last):
            nc.scalar.activation(m_listed[:, j, :], member_planes[j][0][:].indirect(rows3[:]), COPY)
        for planes in (slice(0, 2), slice(2, last)):
            nc.vector.tensor_tensor(y[:, planes, :], m_listed[:, planes, :], o_gain[:, planes, :], ALU.add)
            nc.sync.dma_start(y_rows[:, planes, :], y[:, planes, :])
        y_grouped = keep([P, Q * PACK], BF16, "y_grouped")
        y_codes = keep([P, Q], U32, "y_codes")
        y_scales = keep([P, Q], U8, "y_scales")
        for h, cols in enumerate(halves):
            nc.vector.tensor_tensor(
                y[:, last, cols],
                member_planes[last][0][:].indirect(rows3[:, h * HALF // 16 : (h + 1) * HALF // 16]),
                o_gain[:, last, cols],
                ALU.add,
            )
        nc.sync.dma_start(y_rows[:, last, :], y[:, last, :])
        for cols, copy in zip(halves, (nc.scalar.copy, nc.vector.tensor_copy)):
            copy(
                y_grouped[:, cols.start * PACK : cols.stop * PACK].rearrange("p (c i j) -> p c j i", i=RUN, j=PACK),
                y[:, :, cols].rearrange("p j (c i) -> p c j i", i=RUN),
            )
        for cols in halves:
            nc.vector.quantize_mx(
                out=y_codes[:, cols].bitcast(FP8X4),
                scales=y_scales[:, cols],
                in_=y_grouped[:, cols.start * PACK : cols.stop * PACK],
            )
        nc.sync.dma_start(out_1[0].rearrange("p c t -> p (c t)").bitcast(I32), y_codes[:].bitcast(I32))
        for quad in range(4):
            queue = nc.scalar if quad % 2 == 0 else nc.sync
            queue.dma_start(
                out_2[0, 4 * quad : 4 * quad + 4, :].bitcast(I32),
                y_scales[32 * quad : 32 * quad + 4, :].bitcast(I32),
            )
